import numpy as np
import ml_dtypes


def mxq(x, axis, fmt="e4m3"):
    dtype, down = {"e4m3": (ml_dtypes.float8_e4m3fn, 7), "e5m2": (ml_dtypes.float8_e5m2, 14)}[fmt]
    v = np.moveaxis(np.asarray(x, np.float32).astype(ml_dtypes.bfloat16).astype(np.float64), axis, -1)
    blocks = v.reshape(v.shape[:-1] + (-1, 32))
    amax = np.abs(blocks).max(-1, keepdims=True)
    byte = np.maximum(np.where(amax > 0, np.frexp(amax)[1] - 1 + 127, 0) - down, 1)
    scale = np.exp2(byte - 127.0)
    codes = (blocks / scale).astype(np.float32).astype(dtype).astype(np.float64)
    return np.moveaxis((codes * scale).reshape(v.shape), -1, axis)


WIDE = False


def mx_kscale(k):
    if not WIDE:
        return np.ones(k)
    levels = np.array([10, -10, 5, -5, 0])
    if k % 512:
        return np.exp2(np.random.permutation(np.resize(levels, k // 32))).repeat(32)
    a = np.empty((k // 512, 16))
    for p in range(k // 512):
        a[p, :8] = np.random.permutation(np.resize(levels, 8))
        for g in range(8):
            far = levels[np.abs(levels - a[p, g]) >= 10]
            a[p, g + 8] = far[np.random.randint(len(far))]
    return np.exp2(a.ravel()).repeat(32)


def f64(x):
    return np.asarray(x).astype(np.float64)


def striped(idx):
    return np.tile(idx.reshape(-1, 16).T, (8, 1)).astype(np.uint16)


def unstriped(offs):
    return offs[:16].T.reshape(-1).astype(np.int64)


def silu(v):
    return v / (1.0 + np.exp(-np.maximum(v, -700.0)))


K, T, E, C, H, N = 1536, 1024, 2, 256, 512, 384


def by_expert(wq, xq):
    return np.concatenate([wq[e].T @ xq[:, e * C:(e + 1) * C] for e in range(E)], axis=1)


def setup_inputs():
    n = np.random.standard_normal
    s = mx_kscale(K)[:, None]
    u = mx_kscale(H)
    return {
        "xT": (n((K, T)) * s).astype(np.float32),
        "xr": n((N, T)).astype(np.float32),
        "w1": (n((E, K, H)) / np.sqrt(K) / s[None]).astype(np.float32),
        "w3": (n((E, K, H)) / np.sqrt(K) / s[None] * u[None, None, :]).astype(np.float32),
        "w2": (n((E, H, N)) / np.sqrt(H) / u[None, :, None]).astype(np.float32),
        "gate": np.tile(np.random.uniform(0.2, 1.0, E * C), (N, 1)).astype(np.float32),
        "offs": striped(np.random.permutation(T)[:E * C]),
    }


def reference(xT, xr, w1, w3, w2, gate, offs):
    idx = unstriped(offs)
    xq = mxq(f64(xT)[:, idx], 0, "e4m3")
    h = silu(by_expert(mxq(f64(w1), 1, "e4m3"), xq))
    h = h * by_expert(mxq(f64(w3), 1, "e4m3"), xq)
    y = by_expert(mxq(f64(w2), 1, "e4m3"), mxq(h, 0, "e4m3"))
    out = f64(xr).copy()
    out[:, idx] += f64(gate) * y
    return out

@@ -1,0 +1,287 @@
+from contextlib import ExitStack
+
+import concourse.mybir as mybir
+
+K, T, E, C, H, N = 1536, 1024, 2, 256, 512, 384
+
+F32 = mybir.dt.float32
+BF16 = mybir.dt.bfloat16
+U32 = mybir.dt.uint32
+U16 = mybir.dt.uint16
+U8 = mybir.dt.uint8
+FP8X4 = mybir.dt.float8_e4m3fn_x4
+MULT, ADD = mybir.AluOpType.mult, mybir.AluOpType.add
+SILU = mybir.ActivationFunctionType.Silu
+
+P = 128
+PACK = 4
+PASSES = K // (P * PACK)
+GROUPS = H // P
+SLOTS = E * C
+HALF = C // 2
+N_TILES = N // P
+
+FLOPS = 2 * SLOTS * (2 * K * H + H * N)
+BYTES = 4 * (K * T + 2 * N * T + E * (2 * K * H + H * N) + SLOTS) + 2 * P * SLOTS // 16
+
+
+def tile_moe_res_glu_silu_kernel(tc, xT, xr, w1, w3, w2, gate, offs, out):
+    nc = tc.nc
+    with ExitStack() as ctx:
+        keep = ctx.enter_context(tc.tile_pool(name="keep", bufs=1))
+        xraw_pool = ctx.enter_context(tc.tile_pool(name="xraw", bufs=3))
+        raw_pool = ctx.enter_context(tc.tile_pool(name="raw", bufs=6))
+        stage = ctx.enter_context(tc.tile_pool(name="stage", bufs=6))
+        mid = ctx.enter_context(tc.tile_pool(name="mid", bufs=2))
+        psum = ctx.enter_context(tc.psum_pool(name="psum", bufs=1))
+
+        offsets = keep.tile([P, SLOTS // 16], U16, name="offsets")
+        nc.sync.dma_start(offsets[:], offs)
+
+        warm = keep.tile([P, 1], F32, name="warm")
+        nc.gpsimd.memset(warm[:], 0.0)
+        warm_out = keep.tile([P, 1], F32, name="warm_out")
+        nc.scalar.activation(warm_out[:], warm[:], SILU)
+
+        x_words = [keep.tile([P, T], U32, name=f"x_words{s}", align_bytes=64) for s in range(PASSES)]
+        x_scales = keep.tile([P, T], U8, name="x_scales", align_bytes=64)
+        nc.gpsimd.memset(x_scales[:], 0)
+        windows = [keep.tile([P, T], F32, name=f"window{m}") for m in range(N_TILES)]
+        for m in range(N_TILES):
+            nc.gpsimd.memset(windows[m][:], 0.0)
+        g_words = [keep.tile([P, SLOTS], U32, name=f"g_words{s}", align_bytes=64) for s in range(PASSES)]
+        g_scales = keep.tile([P, SLOTS], U8, name="g_scales", align_bytes=64)
+
+        weights = {"w1": w1, "w3": w3}
+        codes, scales = {}, {}
+        raws, staged = {}, {}
+
+        def load(key):
+            if key[0] == "x":
+                s, parts = key[1], (4 if key[1] == 0 else 1)
+                raw = xraw_pool.tile([P, PACK, T], F32, name="xraw")
+                for i in range(parts):
+                    cols = slice(i * T // parts, (i + 1) * T // parts)
+                    nc.sync.dma_start(raw[:, :, cols], xT[s * 512 : (s + 1) * 512, cols].rearrange("(p j) t -> p j t", j=PACK))
+            else:
+                name, e, s = key
+                raw = raw_pool.tile([P, PACK, H], F32, name="raw")
+                nc.sync.dma_start(raw[:], weights[name][e, s * 512 : (s + 1) * 512, :].rearrange("(p j) c -> p j c", j=PACK))
+            raws[key] = raw
+
+        def copy_x(s, a, b, eng):
+            grouped = stage.tile([P, (b - a) * PACK], BF16, name="grouped", align_bytes=64)
+            src = raws[("x", s)][:, :, a:b].rearrange("p j (c i) -> p c j i", i=4)
+            dst = grouped[:].rearrange("p (c i j) -> p c j i", i=4, j=PACK)
+            if eng == "v":
+                nc.vector.tensor_copy(dst, src)
+            else:
+                nc.scalar.copy(dst, src)
+            staged[("x", s, a)] = grouped
+
+        def quant_x(s, a, b):
+            cols = slice(a, b)
+            nc.vector.quantize_mx(out=x_words[s][:, cols].bitcast(FP8X4), scales=x_scales[4 * s : P, cols], in_=staged[("x", s, a)][:])
+
+        def next_load():
+            if pending:
+                pending.pop(0)()
+
+        def copy_w(key, eng, m0=0, m1=P):
+            if key not in staged:
+                staged[key] = stage.tile([P, 2048], BF16, name="grouped", align_bytes=64)
+            src = raws[key][:].rearrange("p j (m t) -> p m j t", t=GROUPS)[:, m0:m1]
+            dst = staged[key][:].rearrange("p (t m j) -> p m j t", t=GROUPS, j=PACK)[:, m0:m1]
+            if eng == "v":
+                nc.vector.tensor_copy(dst, src)
+            else:
+                nc.scalar.copy(dst, src)
+            if m1 == P:
+                next_load()
+
+        def quant_w(key, pieces=1):
+            codes[key] = keep.tile([P, H], U32, name="codes_%s_%d_%d" % key, align_bytes=64)
+            scales[key] = keep.tile([P, H], U8, name="scales_%s_%d_%d" % key, align_bytes=64)
+            width = H // pieces
+            for i in range(pieces):
+                cols = slice(i * width, (i + 1) * width)
+                nc.vector.quantize_mx(
+                    out=codes[key][:, cols].bitcast(FP8X4), scales=scales[key][:, cols], in_=staged[key][:, 4 * i * width : 4 * (i + 1) * width]
+                )
+
+        w2_raw, w2_codes, w2_scales = {}, {}, {}
+
+        def load_w2(e):
+            w2_raw[e] = keep.tile([P, PACK, N], F32, name=f"w2_raw{e}")
+            nc.sync.dma_start(w2_raw[e][:], w2[e].rearrange("(p j) n -> p j n", j=PACK))
+
+        def prep_w2(e, eng):
+            grouped = keep.tile([P, N * PACK], BF16, name=f"w2_grouped{e}", align_bytes=64)
+            src = w2_raw[e][:].rearrange("p j (c i) -> p c j i", i=4)
+            dst = grouped[:].rearrange("p (c i j) -> p c j i", i=4, j=PACK)
+            if eng == "v":
+                nc.vector.tensor_copy(dst, src)
+            else:
+                nc.scalar.copy(dst, src)
+            w2_codes[e] = keep.tile([P, N], U32, name=f"w2_codes{e}", align_bytes=64)
+            w2_scales[e] = keep.tile([P, N], U8, name=f"w2_scales{e}", align_bytes=64)
+            for a, b in ((0, 256), (256, 384)):
+                nc.vector.quantize_mx(out=w2_codes[e][:, a:b].bitcast(FP8X4), scales=w2_scales[e][:, a:b], in_=grouped[:, 4 * a : 4 * b])
+
+        def gather_words(s):
+            nc.vector.tensor_copy(g_words[s][:], x_words[s][:].indirect(offsets[:]))
+
+        def gather_scales():
+            nc.vector.tensor_copy(g_scales[:], x_scales[:].indirect(offsets[:]))
+
+        def first_layer(name, e, half):
+            bank = psum.tile([P, GROUPS, HALF], F32, name=f"{name}_bank{half}")
+            cols = slice(e * C + half * HALF, e * C + (half + 1) * HALF)
+            for t in range(GROUPS):
+                stat = slice(t * P, (t + 1) * P)
+                for s in range(PASSES):
+                    nc.tensor.matmul_mx(
+                        out=bank[:, t, :],
+                        lhsT=codes[(name, e, s)][:, stat].bitcast(FP8X4),
+                        lhsT_scale=scales[(name, e, s)][:, stat],
+                        rhs=g_words[s][:, cols].bitcast(FP8X4),
+                        rhs_scale=g_scales[4 * s : P, cols],
+                        start=(s == 0),
+                        stop=(s == PASSES - 1),
+                    )
+            return bank
+
+        def silu_of(bank):
+            act = mid.tile([P, HALF, GROUPS], F32, name="act")
+            nc.scalar.activation(act[:], bank[:].rearrange("p t n -> p n t"), SILU)
+            return act
+
+        def hidden(act, bank):
+            hb = mid.tile([P, HALF, GROUPS], BF16, name="hb", align_bytes=64)
+            nc.vector.tensor_tensor(hb[:], bank[:].rearrange("p t n -> p n t"), act[:], MULT)
+            return hb
+
+        def quant_h(hb):
+            hc = mid.tile([P, HALF], U32, name="hc", align_bytes=64)
+            hs = mid.tile([P, HALF], U8, name="hs", align_bytes=64)
+            nc.vector.quantize_mx(out=hc[:].bitcast(FP8X4), scales=hs[:], in_=hb[:].rearrange("p n t -> p (n t)"))
+            return hc, hs
+
+        def second_layer(e, h, m):
+            bank = psum.tile([P, C], F32, name=f"y_bank{m}")
+            stat = slice(m * P, (m + 1) * P)
+            for half in range(2):
+                nc.tensor.matmul_mx(
+                    out=bank[:, half * HALF : (half + 1) * HALF],
+                    lhsT=w2_codes[e][:, stat].bitcast(FP8X4),
+                    lhsT_scale=w2_scales[e][:, stat],
+                    rhs=h[half][0][:].bitcast(FP8X4),
+                    rhs_scale=h[half][1][:],
+                    start=True,
+                    stop=True,
+                )
+            return bank
+
+        def gated(e, m, bank):
+            yg = mid.tile([P, C], F32, name=f"yg{m}")
+            nc.vector.tensor_tensor(yg[:], bank[:], gate_sb[:, e * C : (e + 1) * C], MULT)
+            return yg
+
+        def scatter(e, m, yg):
+            nc.vector.tensor_copy(windows[m][:].indirect(offsets[:, e * C // 16 : (e + 1) * C // 16]), yg[:])
+
+        def finish(m, parts=1):
+            for i in range(parts):
+                cols = slice(i * T // parts, (i + 1) * T // parts)
+                nc.vector.tensor_tensor(xres[m][:, cols], windows[m][:, cols], xres[m][:, cols], ADD)
+                nc.sync.dma_start(out[m * P : (m + 1) * P, cols], xres[m][:, cols])
+
+        gate_sb = keep.tile([P, SLOTS], F32, name="gate_sb")
+        xres = [keep.tile([P, T], F32, name=f"xres{m}") for m in range(N_TILES)]
+        pending = []
+        for s in range(PASSES):
+            load(("x", s))
+            load(("w1", 0, s))
+        for s in range(PASSES):
+            load(("w3", 0, s))
+        load_w2(0)
+        nc.sync.dma_start(gate_sb[:], gate[0:P, :])
+
+        def last_loads():
+            load(("w3", 1, 2))
+            load_w2(1)
+            for m in range(N_TILES):
+                nc.sync.dma_start(xres[m][:], xr[m * P : (m + 1) * P, :])
+
+        pending = [lambda key=key: load(key) for key in (("w1", 1, 0), ("w1", 1, 1), ("w1", 1, 2), ("w3", 1, 0), ("w3", 1, 1))]
+        pending.append(last_loads)
+
+        for i in range(4):
+            copy_x(0, i * 256, (i + 1) * 256, "vsvs"[i])
+        for i in range(4):
+            quant_x(0, i * 256, (i + 1) * 256)
+        copy_w(("w1", 0, 0), "s")
+        copy_x(1, 0, 512, "v")
+        copy_x(1, 512, 1024, "s")
+        gather_words(0)
+        quant_w(("w1", 0, 0))
+        quant_x(1, 0, 512)
+        quant_x(1, 512, 1024)
+        copy_w(("w1", 0, 1), "s")
+        copy_x(2, 0, 512, "v")
+        copy_x(2, 512, 1024, "s")
+        gather_words(1)
+        quant_w(("w1", 0, 1))
+        quant_x(2, 0, 512)
+        quant_x(2, 512, 1024)
+        copy_w(("w1", 0, 2), "s")
+        copy_w(("w3", 0, 0), "s")
+        gather_words(2)
+        quant_w(("w1", 0, 2))
+        gather_scales()
+        copy_w(("w3", 0, 1), "v")
+        quant_w(("w3", 0, 0))
+        copy_w(("w3", 0, 2), "s")
+        quant_w(("w3", 0, 1))
+        quant_w(("w3", 0, 2))
+
+        def expert_middle(e):
+            acts = [silu_of(a_banks[half]) for half in range(2)]
+            g_banks = [first_layer("w3", e, half) for half in range(2)]
+            hbs = [hidden(acts[half], g_banks[half]) for half in range(2)]
+            return [quant_h(hbs[half]) for half in range(2)]
+
+        a_banks = [first_layer("w1", 0, half) for half in range(2)]
+        h = expert_middle(0)
+        prep_w2(0, "s")
+        banks = [second_layer(0, h, m) for m in range(N_TILES)]
+
+        copy_w(("w1", 1, 0), "s")
+        ygs = [gated(0, m, banks[m]) for m in range(N_TILES)]
+        quant_w(("w1", 1, 0))
+        copy_w(("w1", 1, 1), "v")
+        scatter(0, 0, ygs[0])
+        quant_w(("w1", 1, 1))
+        copy_w(("w1", 1, 2), "s")
+        scatter(0, 1, ygs[1])
+        quant_w(("w1", 1, 2))
+        a_banks = [first_layer("w1", 1, half) for half in range(2)]
+        copy_w(("w3", 1, 0), "s")
+        scatter(0, 2, ygs[2])
+        quant_w(("w3", 1, 0))
+        copy_w(("w3", 1, 1), "v")
+        quant_w(("w3", 1, 1))
+        copy_w(("w3", 1, 2), "v", 0, 80)
+        copy_w(("w3", 1, 2), "s", 80, P)
+        quant_w(("w3", 1, 2), pieces=4)
+        h = expert_middle(1)
+        prep_w2(1, "s")
+        banks = [second_layer(1, h, m) for m in range(N_TILES)]
+        ygs = [gated(1, m, banks[m]) for m in range(2)]
+        scatter(1, 0, ygs[0])
+        ygs.append(gated(1, 2, banks[2]))
+        scatter(1, 1, ygs[1])
+        finish(0)
+        scatter(1, 2, ygs[2])
+        finish(1)
+        finish(2, parts=2)

@@ -30,7 +30,7 @@ def tile_moe_res_glu_silu_kernel(tc, xT, xr, w1, w3, w2, gate, offs, out):
     with ExitStack() as ctx:
         keep = ctx.enter_context(tc.tile_pool(name="keep", bufs=1))
         xraw_pool = ctx.enter_context(tc.tile_pool(name="xraw", bufs=3))
-        raw_pool = ctx.enter_context(tc.tile_pool(name="raw", bufs=6))
+        raw_pool = ctx.enter_context(tc.tile_pool(name="raw", bufs=8))
         stage = ctx.enter_context(tc.tile_pool(name="stage", bufs=6))
         mid = ctx.enter_context(tc.tile_pool(name="mid", bufs=2))
         psum = ctx.enter_context(tc.psum_pool(name="psum", bufs=1))
@@ -58,7 +58,7 @@ def tile_moe_res_glu_silu_kernel(tc, xT, xr, w1, w3, w2, gate, offs, out):
 
         def load(key):
             if key[0] == "x":
-                s, parts = key[1], (4 if key[1] == 0 else 1)
+                s, parts = key[1], (2 if key[1] == 0 else 1)
                 raw = xraw_pool.tile([P, PACK, T], F32, name="xraw")
                 for i in range(parts):
                     cols = slice(i * T // parts, (i + 1) * T // parts)
@@ -66,7 +66,10 @@ def tile_moe_res_glu_silu_kernel(tc, xT, xr, w1, w3, w2, gate, offs, out):
             else:
                 name, e, s = key
                 raw = raw_pool.tile([P, PACK, H], F32, name="raw")
-                nc.sync.dma_start(raw[:], weights[name][e, s * 512 : (s + 1) * 512, :].rearrange("(p j) c -> p j c", j=PACK))
+                parts = 1
+                for i in range(parts):
+                    cols = slice(i * H // parts, (i + 1) * H // parts)
+                    nc.sync.dma_start(raw[:, :, cols], weights[name][e, s * 512 : (s + 1) * 512, cols].rearrange("(p j) c -> p j c", j=PACK))
             raws[key] = raw
 
         def copy_x(s, a, b, eng):
@@ -112,7 +115,7 @@ def tile_moe_res_glu_silu_kernel(tc, xT, xr, w1, w3, w2, gate, offs, out):
         w2_raw, w2_codes, w2_scales = {}, {}, {}
 
         def load_w2(e):
-            w2_raw[e] = keep.tile([P, PACK, N], F32, name=f"w2_raw{e}")
+            w2_raw[e] = raw_pool.tile([P, PACK, N], F32, name="raw") if e == 1 else keep.tile([P, PACK, N], F32, name="w2_raw0")
             nc.sync.dma_start(w2_raw[e][:], w2[e].rearrange("(p j) n -> p j n", j=PACK))
 
         def prep_w2(e, eng):
@@ -167,28 +170,27 @@ def tile_moe_res_glu_silu_kernel(tc, xT, xr, w1, w3, w2, gate, offs, out):
             nc.vector.quantize_mx(out=hc[:].bitcast(FP8X4), scales=hs[:], in_=hb[:].rearrange("p n t -> p (n t)"))
             return hc, hs
 
-        def second_layer(e, h, m):
-            bank = psum.tile([P, C], F32, name=f"y_bank{m}")
-            stat = slice(m * P, (m + 1) * P)
-            for half in range(2):
+        def second_layer(e, h, half):
+            bank = psum.tile([P, N_TILES, HALF], F32, name=f"y_bank{half}")
+            for m in range(N_TILES):
+                stat = slice(m * P, (m + 1) * P)
                 nc.tensor.matmul_mx(
-                    out=bank[:, half * HALF : (half + 1) * HALF],
+                    out=bank[:, m, :],
                     lhsT=w2_codes[e][:, stat].bitcast(FP8X4),
                     lhsT_scale=w2_scales[e][:, stat],
-                    rhs=h[half][0][:].bitcast(FP8X4),
-                    rhs_scale=h[half][1][:],
+                    rhs=h[0][:].bitcast(FP8X4),
+                    rhs_scale=h[1][:],
                     start=True,
                     stop=True,
                 )
             return bank
 
-        def gated(e, m, bank):
-            yg = mid.tile([P, C], F32, name=f"yg{m}")
-            nc.vector.tensor_tensor(yg[:], bank[:], gate_sb[:, e * C : (e + 1) * C], MULT)
-            return yg
+        def take_y(y, half, bank):
+            nc.scalar.activation(y[:, :, half * HALF : (half + 1) * HALF], bank[:], mybir.ActivationFunctionType.Copy)
 
-        def scatter(e, m, yg):
-            nc.vector.tensor_copy(windows[m][:].indirect(offsets[:, e * C // 16 : (e + 1) * C // 16]), yg[:])
+        def scatter(e, m, y, a=0, b=C):
+            slots = slice(e * C + a, e * C + b)
+            nc.vector.tensor_tensor(windows[m][:].indirect(offsets[:, slots.start // 16 : slots.stop // 16]), y[:, m, a:b], gate_sb[:, slots], MULT)
 
         def finish(m, parts=1):
             for i in range(parts):
@@ -197,8 +199,17 @@ def tile_moe_res_glu_silu_kernel(tc, xT, xr, w1, w3, w2, gate, offs, out):
                 nc.sync.dma_start(out[m * P : (m + 1) * P, cols], xres[m][:, cols])
 
         gate_sb = keep.tile([P, SLOTS], F32, name="gate_sb")
-        xres = [keep.tile([P, T], F32, name=f"xres{m}") for m in range(N_TILES)]
-        pending = []
+        xres = []
+
+        def last_loads():
+            load_w2(1)
+            for m in range(N_TILES):
+                res = raw_pool.tile([P, T], F32, name="raw")
+                nc.sync.dma_start(res[:], xr[m * P : (m + 1) * P, :])
+                xres.append(res)
+
+        pending = [lambda key=key: load(key) for key in (("w1", 1, 2), ("w3", 1, 0), ("w3", 1, 1), ("w3", 1, 2))]
+        pending.append(last_loads)
         for s in range(PASSES):
             load(("x", s))
             load(("w1", 0, s))
@@ -206,20 +217,13 @@ def tile_moe_res_glu_silu_kernel(tc, xT, xr, w1, w3, w2, gate, offs, out):
             load(("w3", 0, s))
         load_w2(0)
         nc.sync.dma_start(gate_sb[:], gate[0:P, :])
+        load(("w1", 1, 0))
+        load(("w1", 1, 1))
 
-        def last_loads():
-            load(("w3", 1, 2))
-            load_w2(1)
-            for m in range(N_TILES):
-                nc.sync.dma_start(xres[m][:], xr[m * P : (m + 1) * P, :])
-
-        pending = [lambda key=key: load(key) for key in (("w1", 1, 0), ("w1", 1, 1), ("w1", 1, 2), ("w3", 1, 0), ("w3", 1, 1))]
-        pending.append(last_loads)
-
-        for i in range(4):
-            copy_x(0, i * 256, (i + 1) * 256, "vsvs"[i])
-        for i in range(4):
-            quant_x(0, i * 256, (i + 1) * 256)
+        copy_x(0, 0, 512, "v")
+        copy_x(0, 512, 1024, "s")
+        quant_x(0, 0, 512)
+        quant_x(0, 512, 1024)
         copy_w(("w1", 0, 0), "s")
         copy_x(1, 0, 512, "v")
         copy_x(1, 512, 1024, "s")
@@ -241,47 +245,56 @@ def tile_moe_res_glu_silu_kernel(tc, xT, xr, w1, w3, w2, gate, offs, out):
         gather_scales()
         copy_w(("w3", 0, 1), "v")
         quant_w(("w3", 0, 0))
-        copy_w(("w3", 0, 2), "s")
+        copy_w(("w3", 0, 2), "v", 0, 64)
+        copy_w(("w3", 0, 2), "s", 64, P)
         quant_w(("w3", 0, 1))
         quant_w(("w3", 0, 2))
 
-        def expert_middle(e):
-            acts = [silu_of(a_banks[half]) for half in range(2)]
-            g_banks = [first_layer("w3", e, half) for half in range(2)]
-            hbs = [hidden(acts[half], g_banks[half]) for half in range(2)]
-            return [quant_h(hbs[half]) for half in range(2)]
+        def layer(name, e):
+            return [first_layer(name, e, half) for half in range(2)]
 
-        a_banks = [first_layer("w1", 0, half) for half in range(2)]
-        h = expert_middle(0)
+        ys = [mid.tile([P, N_TILES, C], F32, name="y") for e in range(E)]
+
+        a_banks = layer("w1", 0)
+        acts = [silu_of(bank) for bank in a_banks]
+        g_banks = layer("w3", 0)
+        hbs = [hidden(acts[half], g_banks[half]) for half in range(2)]
+        hs = [quant_h(hb) for hb in hbs]
         prep_w2(0, "s")
-        banks = [second_layer(0, h, m) for m in range(N_TILES)]
+        y_banks = [second_layer(0, hs[half], half) for half in range(2)]
 
         copy_w(("w1", 1, 0), "s")
-        ygs = [gated(0, m, banks[m]) for m in range(N_TILES)]
+        for half in range(2):
+            take_y(ys[0], half, y_banks[half])
         quant_w(("w1", 1, 0))
         copy_w(("w1", 1, 1), "v")
-        scatter(0, 0, ygs[0])
+        scatter(0, 0, ys[0])
         quant_w(("w1", 1, 1))
         copy_w(("w1", 1, 2), "s")
-        scatter(0, 1, ygs[1])
+        scatter(0, 1, ys[0])
         quant_w(("w1", 1, 2))
-        a_banks = [first_layer("w1", 1, half) for half in range(2)]
+        a_banks = layer("w1", 1)
         copy_w(("w3", 1, 0), "s")
-        scatter(0, 2, ygs[2])
+        acts = [silu_of(bank) for bank in a_banks]
+        scatter(0, 2, ys[0])
         quant_w(("w3", 1, 0))
         copy_w(("w3", 1, 1), "v")
         quant_w(("w3", 1, 1))
-        copy_w(("w3", 1, 2), "v", 0, 80)
-        copy_w(("w3", 1, 2), "s", 80, P)
+        copy_w(("w3", 1, 2), "s", 0, 64)
+        copy_w(("w3", 1, 2), "v", 64, P)
         quant_w(("w3", 1, 2), pieces=4)
-        h = expert_middle(1)
+        g_banks = layer("w3", 1)
+        hbs = [hidden(acts[half], g_banks[half]) for half in range(2)]
+        hs = [quant_h(hb) for hb in hbs]
         prep_w2(1, "s")
-        banks = [second_layer(1, h, m) for m in range(N_TILES)]
-        ygs = [gated(1, m, banks[m]) for m in range(2)]
-        scatter(1, 0, ygs[0])
-        ygs.append(gated(1, 2, banks[2]))
-        scatter(1, 1, ygs[1])
+        y_banks = [second_layer(1, hs[half], half) for half in range(2)]
+        for half in range(2):
+            take_y(ys[1], half, y_banks[half])
+        for half in range(2):
+            for m in range(2):
+                scatter(1, m, ys[1], half * HALF, (half + 1) * HALF)
+        scatter(1, 2, ys[1], 0, HALF)
         finish(0)
-        scatter(1, 2, ygs[2])
+        scatter(1, 2, ys[1], HALF, C)
         finish(1)
         finish(2, parts=2)

@@ -11,15 +11,18 @@ U16 = mybir.dt.uint16
 U8 = mybir.dt.uint8
 FP8X4 = mybir.dt.float8_e4m3fn_x4
 MULT, ADD = mybir.AluOpType.mult, mybir.AluOpType.add
-SILU = mybir.ActivationFunctionType.Silu
+SILU, COPY = mybir.ActivationFunctionType.Silu, mybir.ActivationFunctionType.Copy
 
 P = 128
 PACK = 4
-PASSES = K // (P * PACK)
-GROUPS = H // P
+K_PASS = P * PACK
+PASSES = K // K_PASS
+H_TILES = H // P
+N_TILES = N // P
 SLOTS = E * C
 HALF = C // 2
-N_TILES = N // P
+RUN = 4
+T_HALF = T // 2
 
 FLOPS = 2 * SLOTS * (2 * K * H + H * N)
 BYTES = 4 * (K * T + 2 * N * T + E * (2 * K * H + H * N) + SLOTS) + 2 * P * SLOTS // 16
@@ -27,9 +30,10 @@ BYTES = 4 * (K * T + 2 * N * T + E * (2 * K * H + H * N) + SLOTS) + 2 * P * SLOT
 
 def tile_moe_res_glu_silu_kernel(tc, xT, xr, w1, w3, w2, gate, offs, out):
     nc = tc.nc
+    by_vector, by_scalar = nc.vector.tensor_copy, nc.scalar.copy
     with ExitStack() as ctx:
         keep = ctx.enter_context(tc.tile_pool(name="keep", bufs=1))
-        xraw_pool = ctx.enter_context(tc.tile_pool(name="xraw", bufs=3))
+        token_pool = ctx.enter_context(tc.tile_pool(name="tokens", bufs=PASSES))
         raw_pool = ctx.enter_context(tc.tile_pool(name="raw", bufs=8))
         stage = ctx.enter_context(tc.tile_pool(name="stage", bufs=6))
         mid = ctx.enter_context(tc.tile_pool(name="mid", bufs=2))
@@ -49,252 +53,225 @@ def tile_moe_res_glu_silu_kernel(tc, xT, xr, w1, w3, w2, gate, offs, out):
         windows = [keep.tile([P, T], F32, name=f"window{m}") for m in range(N_TILES)]
         for m in range(N_TILES):
             nc.gpsimd.memset(windows[m][:], 0.0)
-        g_words = [keep.tile([P, SLOTS], U32, name=f"g_words{s}", align_bytes=64) for s in range(PASSES)]
-        g_scales = keep.tile([P, SLOTS], U8, name="g_scales", align_bytes=64)
-
-        weights = {"w1": w1, "w3": w3}
-        codes, scales = {}, {}
-        raws, staged = {}, {}
-
-        def load(key):
-            if key[0] == "x":
-                s, parts = key[1], (2 if key[1] == 0 else 1)
-                raw = xraw_pool.tile([P, PACK, T], F32, name="xraw")
-                for i in range(parts):
-                    cols = slice(i * T // parts, (i + 1) * T // parts)
-                    nc.sync.dma_start(raw[:, :, cols], xT[s * 512 : (s + 1) * 512, cols].rearrange("(p j) t -> p j t", j=PACK))
-            else:
-                name, e, s = key
-                raw = raw_pool.tile([P, PACK, H], F32, name="raw")
-                parts = 1
-                for i in range(parts):
-                    cols = slice(i * H // parts, (i + 1) * H // parts)
-                    nc.sync.dma_start(raw[:, :, cols], weights[name][e, s * 512 : (s + 1) * 512, cols].rearrange("(p j) c -> p j c", j=PACK))
-            raws[key] = raw
-
-        def copy_x(s, a, b, eng):
-            grouped = stage.tile([P, (b - a) * PACK], BF16, name="grouped", align_bytes=64)
-            src = raws[("x", s)][:, :, a:b].rearrange("p j (c i) -> p c j i", i=4)
-            dst = grouped[:].rearrange("p (c i j) -> p c j i", i=4, j=PACK)
-            if eng == "v":
-                nc.vector.tensor_copy(dst, src)
-            else:
-                nc.scalar.copy(dst, src)
-            staged[("x", s, a)] = grouped
-
-        def quant_x(s, a, b):
-            cols = slice(a, b)
-            nc.vector.quantize_mx(out=x_words[s][:, cols].bitcast(FP8X4), scales=x_scales[4 * s : P, cols], in_=staged[("x", s, a)][:])
-
-        def next_load():
-            if pending:
-                pending.pop(0)()
-
-        def copy_w(key, eng, m0=0, m1=P):
-            if key not in staged:
-                staged[key] = stage.tile([P, 2048], BF16, name="grouped", align_bytes=64)
-            src = raws[key][:].rearrange("p j (m t) -> p m j t", t=GROUPS)[:, m0:m1]
-            dst = staged[key][:].rearrange("p (t m j) -> p m j t", t=GROUPS, j=PACK)[:, m0:m1]
-            if eng == "v":
-                nc.vector.tensor_copy(dst, src)
-            else:
-                nc.scalar.copy(dst, src)
-            if m1 == P:
-                next_load()
-
-        def quant_w(key, pieces=1):
-            codes[key] = keep.tile([P, H], U32, name="codes_%s_%d_%d" % key, align_bytes=64)
-            scales[key] = keep.tile([P, H], U8, name="scales_%s_%d_%d" % key, align_bytes=64)
-            width = H // pieces
-            for i in range(pieces):
-                cols = slice(i * width, (i + 1) * width)
-                nc.vector.quantize_mx(
-                    out=codes[key][:, cols].bitcast(FP8X4), scales=scales[key][:, cols], in_=staged[key][:, 4 * i * width : 4 * (i + 1) * width]
-                )
-
-        w2_raw, w2_codes, w2_scales = {}, {}, {}
-
-        def load_w2(e):
-            w2_raw[e] = raw_pool.tile([P, PACK, N], F32, name="raw") if e == 1 else keep.tile([P, PACK, N], F32, name="w2_raw0")
-            nc.sync.dma_start(w2_raw[e][:], w2[e].rearrange("(p j) n -> p j n", j=PACK))
-
-        def prep_w2(e, eng):
-            grouped = keep.tile([P, N * PACK], BF16, name=f"w2_grouped{e}", align_bytes=64)
-            src = w2_raw[e][:].rearrange("p j (c i) -> p c j i", i=4)
-            dst = grouped[:].rearrange("p (c i j) -> p c j i", i=4, j=PACK)
-            if eng == "v":
-                nc.vector.tensor_copy(dst, src)
-            else:
-                nc.scalar.copy(dst, src)
-            w2_codes[e] = keep.tile([P, N], U32, name=f"w2_codes{e}", align_bytes=64)
-            w2_scales[e] = keep.tile([P, N], U8, name=f"w2_scales{e}", align_bytes=64)
-            for a, b in ((0, 256), (256, 384)):
-                nc.vector.quantize_mx(out=w2_codes[e][:, a:b].bitcast(FP8X4), scales=w2_scales[e][:, a:b], in_=grouped[:, 4 * a : 4 * b])
-
-        def gather_words(s):
-            nc.vector.tensor_copy(g_words[s][:], x_words[s][:].indirect(offsets[:]))
-
-        def gather_scales():
-            nc.vector.tensor_copy(g_scales[:], x_scales[:].indirect(offsets[:]))
-
-        def first_layer(name, e, half):
-            bank = psum.tile([P, GROUPS, HALF], F32, name=f"{name}_bank{half}")
-            cols = slice(e * C + half * HALF, e * C + (half + 1) * HALF)
-            for t in range(GROUPS):
-                stat = slice(t * P, (t + 1) * P)
-                for s in range(PASSES):
-                    nc.tensor.matmul_mx(
-                        out=bank[:, t, :],
-                        lhsT=codes[(name, e, s)][:, stat].bitcast(FP8X4),
-                        lhsT_scale=scales[(name, e, s)][:, stat],
-                        rhs=g_words[s][:, cols].bitcast(FP8X4),
-                        rhs_scale=g_scales[4 * s : P, cols],
-                        start=(s == 0),
-                        stop=(s == PASSES - 1),
-                    )
-            return bank
-
-        def silu_of(bank):
-            act = mid.tile([P, HALF, GROUPS], F32, name="act")
-            nc.scalar.activation(act[:], bank[:].rearrange("p t n -> p n t"), SILU)
-            return act
-
-        def hidden(act, bank):
-            hb = mid.tile([P, HALF, GROUPS], BF16, name="hb", align_bytes=64)
-            nc.vector.tensor_tensor(hb[:], bank[:].rearrange("p t n -> p n t"), act[:], MULT)
-            return hb
-
-        def quant_h(hb):
-            hc = mid.tile([P, HALF], U32, name="hc", align_bytes=64)
-            hs = mid.tile([P, HALF], U8, name="hs", align_bytes=64)
-            nc.vector.quantize_mx(out=hc[:].bitcast(FP8X4), scales=hs[:], in_=hb[:].rearrange("p n t -> p (n t)"))
-            return hc, hs
-
-        def second_layer(e, h, half):
-            bank = psum.tile([P, N_TILES, HALF], F32, name=f"y_bank{half}")
-            for m in range(N_TILES):
-                stat = slice(m * P, (m + 1) * P)
-                nc.tensor.matmul_mx(
-                    out=bank[:, m, :],
-                    lhsT=w2_codes[e][:, stat].bitcast(FP8X4),
-                    lhsT_scale=w2_scales[e][:, stat],
-                    rhs=h[0][:].bitcast(FP8X4),
-                    rhs_scale=h[1][:],
-                    start=True,
-                    stop=True,
-                )
-            return bank
-
-        def take_y(y, half, bank):
-            nc.scalar.activation(y[:, :, half * HALF : (half + 1) * HALF], bank[:], mybir.ActivationFunctionType.Copy)
-
-        def scatter(e, m, y, a=0, b=C):
-            slots = slice(e * C + a, e * C + b)
-            nc.vector.tensor_tensor(windows[m][:].indirect(offsets[:, slots.start // 16 : slots.stop // 16]), y[:, m, a:b], gate_sb[:, slots], MULT)
-
-        def finish(m, parts=1):
-            for i in range(parts):
-                cols = slice(i * T // parts, (i + 1) * T // parts)
-                nc.vector.tensor_tensor(xres[m][:, cols], windows[m][:, cols], xres[m][:, cols], ADD)
-                nc.sync.dma_start(out[m * P : (m + 1) * P, cols], xres[m][:, cols])
+        slot_words = [keep.tile([P, SLOTS], U32, name=f"slot_words{s}", align_bytes=64) for s in range(PASSES)]
+        slot_scales = keep.tile([P, SLOTS], U8, name="slot_scales", align_bytes=64)
 
         gate_sb = keep.tile([P, SLOTS], F32, name="gate_sb")
-        xres = []
+        weights = {"w1": w1, "w3": w3}
+        raws, grouped, codes, scales = {}, {}, {}, {}
+        w2_raw, w2_grouped, w2_codes, w2_scales = {}, {}, {}, {}
+        residual = []
 
-        def last_loads():
-            load_w2(1)
+        def load_tokens(s):
+            raws["x", s] = token_pool.tile([P, PACK, T], F32, name="tokens")
+            nc.sync.dma_start(raws["x", s][:], xT[s * K_PASS : (s + 1) * K_PASS, :].rearrange("(p j) t -> p j t", j=PACK))
+
+        def load_chunk(name, e, s):
+            raws[name, e, s] = raw_pool.tile([P, PACK, H], F32, name="raw")
+            rows = weights[name][e, s * K_PASS : (s + 1) * K_PASS, :]
+            nc.sync.dma_start(raws[name, e, s][:], rows.rearrange("(p j) i -> p j i", j=PACK))
+
+        def load_w2(e, pool, name):
+            w2_raw[e] = pool.tile([P, PACK, N], F32, name=name)
+            nc.sync.dma_start(w2_raw[e][:], w2[e].rearrange("(p j) n -> p j n", j=PACK))
+
+        def load_rest():
+            load_w2(1, raw_pool, "raw")
             for m in range(N_TILES):
                 res = raw_pool.tile([P, T], F32, name="raw")
                 nc.sync.dma_start(res[:], xr[m * P : (m + 1) * P, :])
-                xres.append(res)
+                residual.append(res)
 
-        pending = [lambda key=key: load(key) for key in (("w1", 1, 2), ("w3", 1, 0), ("w3", 1, 1), ("w3", 1, 2))]
-        pending.append(last_loads)
+        def copy_tokens(s, first, copy):
+            grouped["x", s, first] = stage.tile([P, T_HALF * PACK], BF16, name="grouped", align_bytes=64)
+            src = raws["x", s][:, :, first : first + T_HALF].rearrange("p j (c i) -> p c j i", i=RUN)
+            copy(grouped["x", s, first][:].rearrange("p (c i j) -> p c j i", i=RUN, j=PACK), src)
+
+        def quantise_tokens(s, first):
+            cols = slice(first, first + T_HALF)
+            nc.vector.quantize_mx(out=x_words[s][:, cols].bitcast(FP8X4), scales=x_scales[4 * s : P, cols], in_=grouped["x", s, first][:])
+
+        def copy_chunk(key, *cuts):
+            grouped[key] = stage.tile([P, H * PACK], BF16, name="grouped", align_bytes=64)
+            src = raws[key][:].rearrange("p j (m t) -> p m j t", t=H_TILES)
+            dst = grouped[key][:].rearrange("p (t m j) -> p m j t", t=H_TILES, j=PACK)
+            for copy, first, end in cuts:
+                copy(dst[:, first:end], src[:, first:end])
+            if later_loads:
+                later_loads.pop(0)()
+
+        def quantise_chunk(key, pieces=1):
+            codes[key] = keep.tile([P, H], U32, name="codes_%s_%d_%d" % key, align_bytes=64)
+            scales[key] = keep.tile([P, H], U8, name="scales_%s_%d_%d" % key, align_bytes=64)
+            width = H // pieces
+            for a in range(0, H, width):
+                cols = slice(a, a + width)
+                source = grouped[key][:, PACK * a : PACK * (a + width)]
+                nc.vector.quantize_mx(out=codes[key][:, cols].bitcast(FP8X4), scales=scales[key][:, cols], in_=source)
+
+        def prepare_w2(e):
+            w2_grouped[e] = keep.tile([P, N * PACK], BF16, name=f"w2_grouped{e}", align_bytes=64)
+            src = w2_raw[e][:].rearrange("p j (c i) -> p c j i", i=RUN)
+            nc.scalar.copy(w2_grouped[e][:].rearrange("p (c i j) -> p c j i", i=RUN, j=PACK), src)
+            w2_codes[e] = keep.tile([P, N], U32, name=f"w2_codes{e}", align_bytes=64)
+            w2_scales[e] = keep.tile([P, N], U8, name=f"w2_scales{e}", align_bytes=64)
+            for a, b in ((0, 256), (256, N)):
+                source = w2_grouped[e][:, PACK * a : PACK * b]
+                nc.vector.quantize_mx(out=w2_codes[e][:, a:b].bitcast(FP8X4), scales=w2_scales[e][:, a:b], in_=source)
+
+        def gather_words(s):
+            nc.vector.tensor_copy(slot_words[s][:], x_words[s][:].indirect(offsets[:]))
+
+        def gather_scales():
+            nc.vector.tensor_copy(slot_scales[:], x_scales[:].indirect(offsets[:]))
+
+        def first_layer(name, e):
+            banks = []
+            for half in range(2):
+                bank = psum.tile([P, H_TILES, HALF], F32, name=f"{name}_bank{half}")
+                slots = slice(e * C + half * HALF, e * C + (half + 1) * HALF)
+                for t in range(H_TILES):
+                    channels = slice(t * P, (t + 1) * P)
+                    for s in range(PASSES):
+                        nc.tensor.matmul_mx(
+                            out=bank[:, t, :],
+                            lhsT=codes[name, e, s][:, channels].bitcast(FP8X4),
+                            lhsT_scale=scales[name, e, s][:, channels],
+                            rhs=slot_words[s][:, slots].bitcast(FP8X4),
+                            rhs_scale=slot_scales[4 * s : P, slots],
+                            start=(s == 0),
+                            stop=(s == PASSES - 1),
+                        )
+                banks.append(bank)
+            return banks
+
+        def silu_of(banks):
+            acts = []
+            for bank in banks:
+                act = mid.tile([P, HALF, H_TILES], F32, name="act")
+                nc.scalar.activation(act[:], bank[:].rearrange("p t n -> p n t"), SILU)
+                acts.append(act)
+            return acts
+
+        def hidden(acts, banks):
+            halves = []
+            for act, bank in zip(acts, banks):
+                h = mid.tile([P, HALF, H_TILES], BF16, name="h", align_bytes=64)
+                nc.vector.tensor_tensor(h[:], bank[:].rearrange("p t n -> p n t"), act[:], MULT)
+                halves.append(h)
+            return halves
+
+        def quantise_hidden(halves):
+            packed = []
+            for h in halves:
+                h_codes = mid.tile([P, HALF], U32, name="h_codes", align_bytes=64)
+                h_scales = mid.tile([P, HALF], U8, name="h_scales", align_bytes=64)
+                nc.vector.quantize_mx(out=h_codes[:].bitcast(FP8X4), scales=h_scales[:], in_=h[:].rearrange("p n t -> p (n t)"))
+                packed.append((h_codes, h_scales))
+            return packed
+
+        def second_layer(e, packed):
+            banks = []
+            for half, (h_codes, h_scales) in enumerate(packed):
+                bank = psum.tile([P, N_TILES, HALF], F32, name=f"y_bank{half}")
+                for m in range(N_TILES):
+                    rows = slice(m * P, (m + 1) * P)
+                    nc.tensor.matmul_mx(
+                        out=bank[:, m, :],
+                        lhsT=w2_codes[e][:, rows].bitcast(FP8X4),
+                        lhsT_scale=w2_scales[e][:, rows],
+                        rhs=h_codes[:].bitcast(FP8X4),
+                        rhs_scale=h_scales[:],
+                        start=True,
+                        stop=True,
+                    )
+                banks.append(bank)
+            return banks
+
+        def take_y(y, banks):
+            for half, bank in enumerate(banks):
+                nc.scalar.activation(y[:, :, half * HALF : (half + 1) * HALF], bank[:], COPY)
+
+        def scatter(e, m, y, a=0, b=C):
+            first, end = e * C + a, e * C + b
+            window = windows[m][:].indirect(offsets[:, first // 16 : end // 16])
+            nc.vector.tensor_tensor(window, y[:, m, a:b], gate_sb[:, first:end], MULT)
+
+        def finish(m, parts=1):
+            width = T // parts
+            for a in range(0, T, width):
+                cols = slice(a, a + width)
+                nc.vector.tensor_tensor(residual[m][:, cols], windows[m][:, cols], residual[m][:, cols], ADD)
+                nc.sync.dma_start(out[m * P : (m + 1) * P, cols], residual[m][:, cols])
+
+        later_loads = [lambda key=key: load_chunk(*key) for key in (("w1", 1, 2), ("w3", 1, 0), ("w3", 1, 1), ("w3", 1, 2))]
+        later_loads.append(load_rest)
         for s in range(PASSES):
-            load(("x", s))
-            load(("w1", 0, s))
+            load_tokens(s)
+            load_chunk("w1", 0, s)
         for s in range(PASSES):
-            load(("w3", 0, s))
-        load_w2(0)
+            load_chunk("w3", 0, s)
+        load_w2(0, keep, "w2_raw0")
         nc.sync.dma_start(gate_sb[:], gate[0:P, :])
-        load(("w1", 1, 0))
-        load(("w1", 1, 1))
+        load_chunk("w1", 1, 0)
+        load_chunk("w1", 1, 1)
 
-        copy_x(0, 0, 512, "v")
-        copy_x(0, 512, 1024, "s")
-        quant_x(0, 0, 512)
-        quant_x(0, 512, 1024)
-        copy_w(("w1", 0, 0), "s")
-        copy_x(1, 0, 512, "v")
-        copy_x(1, 512, 1024, "s")
-        gather_words(0)
-        quant_w(("w1", 0, 0))
-        quant_x(1, 0, 512)
-        quant_x(1, 512, 1024)
-        copy_w(("w1", 0, 1), "s")
-        copy_x(2, 0, 512, "v")
-        copy_x(2, 512, 1024, "s")
-        gather_words(1)
-        quant_w(("w1", 0, 1))
-        quant_x(2, 0, 512)
-        quant_x(2, 512, 1024)
-        copy_w(("w1", 0, 2), "s")
-        copy_w(("w3", 0, 0), "s")
-        gather_words(2)
-        quant_w(("w1", 0, 2))
+        for s in range(PASSES):
+            copy_tokens(s, 0, by_vector)
+            copy_tokens(s, T_HALF, by_scalar)
+            if s > 0:
+                gather_words(s - 1)
+                quantise_chunk(("w1", 0, s - 1))
+            quantise_tokens(s, 0)
+            quantise_tokens(s, T_HALF)
+            copy_chunk(("w1", 0, s), (by_scalar, 0, P))
+        copy_chunk(("w3", 0, 0), (by_scalar, 0, P))
+        gather_words(PASSES - 1)
+        quantise_chunk(("w1", 0, PASSES - 1))
         gather_scales()
-        copy_w(("w3", 0, 1), "v")
-        quant_w(("w3", 0, 0))
-        copy_w(("w3", 0, 2), "v", 0, 64)
-        copy_w(("w3", 0, 2), "s", 64, P)
-        quant_w(("w3", 0, 1))
-        quant_w(("w3", 0, 2))
-
-        def layer(name, e):
-            return [first_layer(name, e, half) for half in range(2)]
+        copy_chunk(("w3", 0, 1), (by_vector, 0, P))
+        quantise_chunk(("w3", 0, 0))
+        copy_chunk(("w3", 0, 2), (by_vector, 0, P // 2), (by_scalar, P // 2, P))
+        quantise_chunk(("w3", 0, 1))
+        quantise_chunk(("w3", 0, 2))
 
         ys = [mid.tile([P, N_TILES, C], F32, name="y") for e in range(E)]
 
-        a_banks = layer("w1", 0)
-        acts = [silu_of(bank) for bank in a_banks]
-        g_banks = layer("w3", 0)
-        hbs = [hidden(acts[half], g_banks[half]) for half in range(2)]
-        hs = [quant_h(hb) for hb in hbs]
-        prep_w2(0, "s")
-        y_banks = [second_layer(0, hs[half], half) for half in range(2)]
+        w1_banks = first_layer("w1", 0)
+        acts = silu_of(w1_banks)
+        packed = quantise_hidden(hidden(acts, first_layer("w3", 0)))
+        prepare_w2(0)
+        y_banks = second_layer(0, packed)
 
-        copy_w(("w1", 1, 0), "s")
-        for half in range(2):
-            take_y(ys[0], half, y_banks[half])
-        quant_w(("w1", 1, 0))
-        copy_w(("w1", 1, 1), "v")
+        copy_chunk(("w1", 1, 0), (by_scalar, 0, P))
+        take_y(ys[0], y_banks)
+        quantise_chunk(("w1", 1, 0))
+        copy_chunk(("w1", 1, 1), (by_vector, 0, P))
         scatter(0, 0, ys[0])
-        quant_w(("w1", 1, 1))
-        copy_w(("w1", 1, 2), "s")
+        quantise_chunk(("w1", 1, 1))
+        copy_chunk(("w1", 1, 2), (by_scalar, 0, P))
         scatter(0, 1, ys[0])
-        quant_w(("w1", 1, 2))
-        a_banks = layer("w1", 1)
-        copy_w(("w3", 1, 0), "s")
-        acts = [silu_of(bank) for bank in a_banks]
+        quantise_chunk(("w1", 1, 2))
+        w1_banks = first_layer("w1", 1)
+        copy_chunk(("w3", 1, 0), (by_scalar, 0, P))
+        acts = silu_of(w1_banks)
         scatter(0, 2, ys[0])
-        quant_w(("w3", 1, 0))
-        copy_w(("w3", 1, 1), "v")
-        quant_w(("w3", 1, 1))
-        copy_w(("w3", 1, 2), "s", 0, 64)
-        copy_w(("w3", 1, 2), "v", 64, P)
-        quant_w(("w3", 1, 2), pieces=4)
-        g_banks = layer("w3", 1)
-        hbs = [hidden(acts[half], g_banks[half]) for half in range(2)]
-        hs = [quant_h(hb) for hb in hbs]
-        prep_w2(1, "s")
-        y_banks = [second_layer(1, hs[half], half) for half in range(2)]
+        quantise_chunk(("w3", 1, 0))
+        copy_chunk(("w3", 1, 1), (by_vector, 0, P))
+        quantise_chunk(("w3", 1, 1))
+        copy_chunk(("w3", 1, 2), (by_scalar, 0, 48), (by_vector, 48, P))
+        quantise_chunk(("w3", 1, 2), pieces=H_TILES)
+        packed = quantise_hidden(hidden(acts, first_layer("w3", 1)))
+        prepare_w2(1)
+        y_banks = second_layer(1, packed)
+        take_y(ys[1], y_banks)
+
         for half in range(2):
-            take_y(ys[1], half, y_banks[half])
-        for half in range(2):
-            for m in range(2):
+            for m in range(N_TILES - 1):
                 scatter(1, m, ys[1], half * HALF, (half + 1) * HALF)
-        scatter(1, 2, ys[1], 0, HALF)
+        last = N_TILES - 1
+        scatter(1, last, ys[1], 0, HALF)
         finish(0)
-        scatter(1, 2, ys[1], HALF, C)
+        scatter(1, last, ys[1], HALF, C)
         finish(1)
-        finish(2, parts=2)
+        finish(last, parts=2)

from contextlib import ExitStack

import concourse.mybir as mybir

K, T, E, C, H, N = 1536, 1024, 2, 256, 512, 384

F32 = mybir.dt.float32
BF16 = mybir.dt.bfloat16
U32 = mybir.dt.uint32
U16 = mybir.dt.uint16
U8 = mybir.dt.uint8
FP8X4 = mybir.dt.float8_e4m3fn_x4
MULT, ADD = mybir.AluOpType.mult, mybir.AluOpType.add
SILU, COPY = mybir.ActivationFunctionType.Silu, mybir.ActivationFunctionType.Copy

P = 128
PACK = 4
K_PASS = P * PACK
PASSES = K // K_PASS
H_TILES = H // P
N_TILES = N // P
SLOTS = E * C
HALF = C // 2
RUN = 4
T_HALF = T // 2

FLOPS = 2 * SLOTS * (2 * K * H + H * N)
BYTES = 4 * (K * T + 2 * N * T + E * (2 * K * H + H * N) + SLOTS) + 2 * P * SLOTS // 16


def tile_moe_res_glu_silu_kernel(tc, xT, xr, w1, w3, w2, gate, offs, out):
    nc = tc.nc
    by_vector, by_scalar = nc.vector.tensor_copy, nc.scalar.copy
    with ExitStack() as ctx:
        keep = ctx.enter_context(tc.tile_pool(name="keep", bufs=1))
        token_pool = ctx.enter_context(tc.tile_pool(name="tokens", bufs=PASSES))
        raw_pool = ctx.enter_context(tc.tile_pool(name="raw", bufs=8))
        stage = ctx.enter_context(tc.tile_pool(name="stage", bufs=6))
        mid = ctx.enter_context(tc.tile_pool(name="mid", bufs=2))
        psum = ctx.enter_context(tc.psum_pool(name="psum", bufs=1))

        offsets = keep.tile([P, SLOTS // 16], U16, name="offsets")
        nc.sync.dma_start(offsets[:], offs)

        warm = keep.tile([P, 1], F32, name="warm")
        nc.gpsimd.memset(warm[:], 0.0)
        warm_out = keep.tile([P, 1], F32, name="warm_out")
        nc.scalar.activation(warm_out[:], warm[:], SILU)

        x_words = [keep.tile([P, T], U32, name=f"x_words{s}", align_bytes=64) for s in range(PASSES)]
        x_scales = keep.tile([P, T], U8, name="x_scales", align_bytes=64)
        nc.gpsimd.memset(x_scales[:], 0)
        windows = [keep.tile([P, T], F32, name=f"window{m}") for m in range(N_TILES)]
        for m in range(N_TILES):
            nc.gpsimd.memset(windows[m][:], 0.0)
        slot_words = [keep.tile([P, SLOTS], U32, name=f"slot_words{s}", align_bytes=64) for s in range(PASSES)]
        slot_scales = keep.tile([P, SLOTS], U8, name="slot_scales", align_bytes=64)

        gate_sb = keep.tile([P, SLOTS], F32, name="gate_sb")
        weights = {"w1": w1, "w3": w3}
        raws, grouped, codes, scales = {}, {}, {}, {}
        w2_raw, w2_grouped, w2_codes, w2_scales = {}, {}, {}, {}
        residual = []

        def load_tokens(s):
            raws["x", s] = token_pool.tile([P, PACK, T], F32, name="tokens")
            nc.sync.dma_start(raws["x", s][:], xT[s * K_PASS : (s + 1) * K_PASS, :].rearrange("(p j) t -> p j t", j=PACK))

        def load_chunk(name, e, s):
            raws[name, e, s] = raw_pool.tile([P, PACK, H], F32, name="raw")
            rows = weights[name][e, s * K_PASS : (s + 1) * K_PASS, :]
            nc.sync.dma_start(raws[name, e, s][:], rows.rearrange("(p j) i -> p j i", j=PACK))

        def load_w2(e, pool, name):
            w2_raw[e] = pool.tile([P, PACK, N], F32, name=name)
            nc.sync.dma_start(w2_raw[e][:], w2[e].rearrange("(p j) n -> p j n", j=PACK))

        def load_rest():
            load_w2(1, raw_pool, "raw")
            for m in range(N_TILES):
                res = raw_pool.tile([P, T], F32, name="raw")
                nc.sync.dma_start(res[:], xr[m * P : (m + 1) * P, :])
                residual.append(res)

        def copy_tokens(s, first, copy):
            grouped["x", s, first] = stage.tile([P, T_HALF * PACK], BF16, name="grouped", align_bytes=64)
            src = raws["x", s][:, :, first : first + T_HALF].rearrange("p j (c i) -> p c j i", i=RUN)
            copy(grouped["x", s, first][:].rearrange("p (c i j) -> p c j i", i=RUN, j=PACK), src)

        def quantise_tokens(s, first):
            cols = slice(first, first + T_HALF)
            nc.vector.quantize_mx(out=x_words[s][:, cols].bitcast(FP8X4), scales=x_scales[4 * s : P, cols], in_=grouped["x", s, first][:])

        def copy_chunk(key, *cuts):
            grouped[key] = stage.tile([P, H * PACK], BF16, name="grouped", align_bytes=64)
            src = raws[key][:].rearrange("p j (m t) -> p m j t", t=H_TILES)
            dst = grouped[key][:].rearrange("p (t m j) -> p m j t", t=H_TILES, j=PACK)
            for copy, first, end in cuts:
                copy(dst[:, first:end], src[:, first:end])
            if later_loads:
                later_loads.pop(0)()

        def quantise_chunk(key, pieces=1):
            codes[key] = keep.tile([P, H], U32, name="codes_%s_%d_%d" % key, align_bytes=64)
            scales[key] = keep.tile([P, H], U8, name="scales_%s_%d_%d" % key, align_bytes=64)
            width = H // pieces
            for a in range(0, H, width):
                cols = slice(a, a + width)
                source = grouped[key][:, PACK * a : PACK * (a + width)]
                nc.vector.quantize_mx(out=codes[key][:, cols].bitcast(FP8X4), scales=scales[key][:, cols], in_=source)

        def prepare_w2(e):
            w2_grouped[e] = keep.tile([P, N * PACK], BF16, name=f"w2_grouped{e}", align_bytes=64)
            src = w2_raw[e][:].rearrange("p j (c i) -> p c j i", i=RUN)
            nc.scalar.copy(w2_grouped[e][:].rearrange("p (c i j) -> p c j i", i=RUN, j=PACK), src)
            w2_codes[e] = keep.tile([P, N], U32, name=f"w2_codes{e}", align_bytes=64)
            w2_scales[e] = keep.tile([P, N], U8, name=f"w2_scales{e}", align_bytes=64)
            for a, b in ((0, 256), (256, N)):
                source = w2_grouped[e][:, PACK * a : PACK * b]
                nc.vector.quantize_mx(out=w2_codes[e][:, a:b].bitcast(FP8X4), scales=w2_scales[e][:, a:b], in_=source)

        def gather_words(s):
            nc.vector.tensor_copy(slot_words[s][:], x_words[s][:].indirect(offsets[:]))

        def gather_scales():
            nc.vector.tensor_copy(slot_scales[:], x_scales[:].indirect(offsets[:]))

        def first_layer(name, e):
            banks = []
            for half in range(2):
                bank = psum.tile([P, H_TILES, HALF], F32, name=f"{name}_bank{half}")
                slots = slice(e * C + half * HALF, e * C + (half + 1) * HALF)
                for t in range(H_TILES):
                    channels = slice(t * P, (t + 1) * P)
                    for s in range(PASSES):
                        nc.tensor.matmul_mx(
                            out=bank[:, t, :],
                            lhsT=codes[name, e, s][:, channels].bitcast(FP8X4),
                            lhsT_scale=scales[name, e, s][:, channels],
                            rhs=slot_words[s][:, slots].bitcast(FP8X4),
                            rhs_scale=slot_scales[4 * s : P, slots],
                            start=(s == 0),
                            stop=(s == PASSES - 1),
                        )
                banks.append(bank)
            return banks

        def silu_of(banks):
            acts = []
            for bank in banks:
                act = mid.tile([P, HALF, H_TILES], F32, name="act")
                nc.scalar.activation(act[:], bank[:].rearrange("p t n -> p n t"), SILU)
                acts.append(act)
            return acts

        def hidden(acts, banks):
            halves = []
            for act, bank in zip(acts, banks):
                h = mid.tile([P, HALF, H_TILES], BF16, name="h", align_bytes=64)
                nc.vector.tensor_tensor(h[:], bank[:].rearrange("p t n -> p n t"), act[:], MULT)
                halves.append(h)
            return halves

        def quantise_hidden(halves):
            packed = []
            for h in halves:
                h_codes = mid.tile([P, HALF], U32, name="h_codes", align_bytes=64)
                h_scales = mid.tile([P, HALF], U8, name="h_scales", align_bytes=64)
                nc.vector.quantize_mx(out=h_codes[:].bitcast(FP8X4), scales=h_scales[:], in_=h[:].rearrange("p n t -> p (n t)"))
                packed.append((h_codes, h_scales))
            return packed

        def second_layer(e, packed):
            banks = []
            for half, (h_codes, h_scales) in enumerate(packed):
                bank = psum.tile([P, N_TILES, HALF], F32, name=f"y_bank{half}")
                for m in range(N_TILES):
                    rows = slice(m * P, (m + 1) * P)
                    nc.tensor.matmul_mx(
                        out=bank[:, m, :],
                        lhsT=w2_codes[e][:, rows].bitcast(FP8X4),
                        lhsT_scale=w2_scales[e][:, rows],
                        rhs=h_codes[:].bitcast(FP8X4),
                        rhs_scale=h_scales[:],
                        start=True,
                        stop=True,
                    )
                banks.append(bank)
            return banks

        def take_y(y, banks):
            for half, bank in enumerate(banks):
                nc.scalar.activation(y[:, :, half * HALF : (half + 1) * HALF], bank[:], COPY)

        def scatter(e, m, y, a=0, b=C):
            first, end = e * C + a, e * C + b
            window = windows[m][:].indirect(offsets[:, first // 16 : end // 16])
            nc.vector.tensor_tensor(window, y[:, m, a:b], gate_sb[:, first:end], MULT)

        def finish(m, parts=1):
            width = T // parts
            for a in range(0, T, width):
                cols = slice(a, a + width)
                nc.vector.tensor_tensor(residual[m][:, cols], windows[m][:, cols], residual[m][:, cols], ADD)
                nc.sync.dma_start(out[m * P : (m + 1) * P, cols], residual[m][:, cols])

        later_loads = [lambda key=key: load_chunk(*key) for key in (("w1", 1, 2), ("w3", 1, 0), ("w3", 1, 1), ("w3", 1, 2))]
        later_loads.append(load_rest)
        for s in range(PASSES):
            load_tokens(s)
            load_chunk("w1", 0, s)
        for s in range(PASSES):
            load_chunk("w3", 0, s)
        load_w2(0, keep, "w2_raw0")
        nc.sync.dma_start(gate_sb[:], gate[0:P, :])
        load_chunk("w1", 1, 0)
        load_chunk("w1", 1, 1)

        for s in range(PASSES):
            copy_tokens(s, 0, by_vector)
            copy_tokens(s, T_HALF, by_scalar)
            if s > 0:
                gather_words(s - 1)
                quantise_chunk(("w1", 0, s - 1))
            quantise_tokens(s, 0)
            quantise_tokens(s, T_HALF)
            copy_chunk(("w1", 0, s), (by_scalar, 0, P))
        copy_chunk(("w3", 0, 0), (by_scalar, 0, P))
        gather_words(PASSES - 1)
        quantise_chunk(("w1", 0, PASSES - 1))
        gather_scales()
        copy_chunk(("w3", 0, 1), (by_vector, 0, P))
        quantise_chunk(("w3", 0, 0))
        copy_chunk(("w3", 0, 2), (by_vector, 0, P // 2), (by_scalar, P // 2, P))
        quantise_chunk(("w3", 0, 1))
        quantise_chunk(("w3", 0, 2))

        ys = [mid.tile([P, N_TILES, C], F32, name="y") for e in range(E)]

        w1_banks = first_layer("w1", 0)
        acts = silu_of(w1_banks)
        packed = quantise_hidden(hidden(acts, first_layer("w3", 0)))
        prepare_w2(0)
        y_banks = second_layer(0, packed)

        copy_chunk(("w1", 1, 0), (by_scalar, 0, P))
        take_y(ys[0], y_banks)
        quantise_chunk(("w1", 1, 0))
        copy_chunk(("w1", 1, 1), (by_vector, 0, P))
        scatter(0, 0, ys[0])
        quantise_chunk(("w1", 1, 1))
        copy_chunk(("w1", 1, 2), (by_scalar, 0, P))
        scatter(0, 1, ys[0])
        quantise_chunk(("w1", 1, 2))
        w1_banks = first_layer("w1", 1)
        copy_chunk(("w3", 1, 0), (by_scalar, 0, P))
        acts = silu_of(w1_banks)
        scatter(0, 2, ys[0])
        quantise_chunk(("w3", 1, 0))
        copy_chunk(("w3", 1, 1), (by_vector, 0, P))
        quantise_chunk(("w3", 1, 1))
        copy_chunk(("w3", 1, 2), (by_scalar, 0, 48), (by_vector, 48, P))
        quantise_chunk(("w3", 1, 2), pieces=H_TILES)
        packed = quantise_hidden(hidden(acts, first_layer("w3", 1)))
        prepare_w2(1)
        y_banks = second_layer(1, packed)
        take_y(ys[1], y_banks)

        for half in range(2):
            for m in range(N_TILES - 1):
                scatter(1, m, ys[1], half * HALF, (half + 1) * HALF)
        last = N_TILES - 1
        scatter(1, last, ys[1], 0, HALF)
        finish(0)
        scatter(1, last, ys[1], HALF, C)
        finish(1)
        finish(last, parts=2)
